import numpy as np, ml_dtypes
CORES = [16,17,18,19,32,33,34,35]
N = 8
BF = ml_dtypes.bfloat16
def gentries(a):
    return np.ascontiguousarray(a.reshape(8, 16, -1).transpose(0, 2, 1)).reshape(8, -1)
def gtable(e):
    e = np.asarray(e); return np.ascontiguousarray(e.reshape(8, -1, 16).transpose(0, 2, 1)).reshape(128, -1).astype(np.int32)
P, M, W, CAP, S, RO = 2048, 4096, 6144, 1024, 5, 3
def parts(rng):
    x = rng.integers(0, 16, (N, 8, 16, W), dtype=np.int16)
    src = rng.integers(0, W, (N, 8, M)); trig = rng.integers(0, W, (N, 8, M))
    tg = np.ascontiguousarray(np.argsort(rng.random((N, 8, W)), axis=-1)[..., :M])
    th = rng.choice(np.array([66, 74, 80, 86, 92]), (N, 8, 1)); th[0, 0] = 66; th[1, 1] = 92
    return x, src, trig, tg, th
def dist(x, trig):
    return np.add.reduce(np.abs(np.take_along_axis(x, trig[:, :, None, :], 3) - x[..., P:]), axis=2)
def aim(rng, x, th, want):
    none = np.zeros((N, 8, M), np.int64)
    t = np.where(want, P + np.arange(M), np.where(dist(x, none) >= dist(x, none + 1), 0, 1))
    for k in range(4):
        c = rng.integers(0, W, (N, 8, M)); t = np.where((dist(x, c) < th) == want, c, t)
    return t
def aimed(rng, e, b):
    o = rng.permutation(W); t = o[~np.isin(o, b)][:M]; t[e] = b
    return t
def apart(rng, n):
    return np.stack([2 * rng.permutation(M // 2)[:n] + rng.integers(0, 2, n) for r in range(N)])
def pack(x, src, trig, tg, th):
    return {"x": x.reshape(N, 128, W).astype(np.float32).astype(BF), "src": np.stack([gtable(a) for a in src]), "trig": np.stack([gtable(a) for a in trig]),
            "tg": np.stack([gtable(a) for a in tg]), "th": np.ascontiguousarray(np.repeat(th, 16, axis=2).reshape(N, 128, 1)).astype(np.int32)}
def setup_inputs(rng):
    return pack(*parts(rng))
def setup_inputs_room(rng):
    x, src, trig, tg, th = parts(rng); x[..., 0] = 0; x[..., 1] = 15
    n = rng.choice(np.array([0, 1, CAP - 1, CAP, CAP + 1, M]), (N, 8)); n[0] = np.array([CAP, CAP + 1, M, CAP - 1, 1, 0, CAP, CAP + 1])
    n[1] = rng.permutation(np.arange(2, 10)); n[2] = rng.permutation(np.arange(10, 18))
    key = rng.random((N, 8, M)); key[0, :, M - 1] = -1.0
    want = np.argsort(np.argsort(key, axis=-1), axis=-1) < n[:, :, None]
    return pack(x, src, aim(rng, x, th, want), tg, th)
def setup_inputs_ties(rng):
    x, src, trig, tg, th = parts(rng)
    lo = rng.choice(np.array([0, 4, 7]), (N, 8, 1, 1)); lo[0, :3] = np.array([0, 4, 7]).reshape(3, 1, 1); lo[1:, 3] = 0; lo[:, 4] = 7
    x = lo + (15 - 2 * lo) * rng.integers(0, 2, (N, 8, 16, W))
    th = 8 * (15 - 2 * lo[..., 0]) + rng.integers(0, 2, (N, 8, 1)); th[0, 3] = 0; th[1, 3] = 241; th[2, 3] = 240; th[3:, 3] = rng.integers(161, 241, (N - 3, 1))
    x[1:, 3, :, 0] = 0; x[1:, 3, :, P:P + 8] = 15; trig[1:, 3, :8] = 0
    th[:, 4] = 1 + (np.arange(N)[:, None] + rng.integers(0, 7)) % 7
    m = x[:, 4, :, P:P + 8]; x[:, 4, :, :8] = np.where(np.arange(16)[:, None] < np.arange(8), 15 - m, m); trig[:, 4, :8] = np.arange(8)
    return pack(x, src, trig, tg, th)
def setup_inputs_alike(rng):
    x, src, trig, tg, th = parts(rng); e = np.arange(M); h = min(P, M - M // 16); low = e % 16 < 8
    for q in range(N):
        tg[q, 0] = P + rng.permutation(M)
        tg[q, 1] = rng.permutation(np.concatenate([rng.permutation(P)[:h], P + rng.permutation(M)[:M - h]]))
        tg[q, 2] = P + (2 * rng.permutation(M // 2)[:, None] + np.array([0, 1])).reshape(-1)
        tg[q, 3, low] = P + 2 * rng.permutation(M // 2); tg[q, 3, ~low] = rng.permutation(P)[:M // 2]
        o = rng.permutation(W); tg[q, 5] = o[np.argsort((o + rng.integers(0, 16)) % 16, kind="stable")][:M]
        tg[q, 7] = e if q % 2 == 0 else W - 1 - e
    x[:, 2, :, P + 1::2] = x[:, 2, :, P::2]; trig[:, 2, 1::2] = trig[:, 2, ::2]
    src[:, 3] = rng.integers(0, P, (N, M)); trig[:, 3] = np.where(low, P + e, rng.integers(0, P, (N, M))); th[:, 3] = 1
    x[:, 4, :, P:] = rng.integers(0, 8, (N, 16, M)); x[:, 5, :, P:] = rng.integers(8, 16, (N, 16, M)); th[:, 5] = 241
    src[:, 6] = rng.choice(np.array([0, W - 1, P - 1, P]), (N, M)); trig[:, 6] = rng.choice(np.array([0, W - 1, P - 1, P]), (N, M))
    trig[:, 7] = P + e; th[:, 7] = 1
    return pack(x, src, trig, tg, th)
def setup_inputs_cold(rng):
    x, src, trig, tg, th = parts(rng); q = rng.permutation(N); g = rng.permutation(8)
    th[q[0]] = 0; th[q[1]] = 241
    th[:, g[:3]] = 0; th[3, g[1]] = 80; th[rng.integers(0, N), g[2]] = 80
    for k in g[3:6]:
        th[:, k] = 1; src[:, k] = rng.integers(0, P, (N, M)); trig[:, k] = rng.integers(0, P, (N, M))
    for k, n in ((g[3], 5), (g[4], int(rng.integers(2, 18)))):
        e = np.sort(apart(rng, n), axis=1)
        for r in range(N):
            trig[r, k, e[r]] = P + e[r]; tg[r, k] = aimed(rng, e[r], P + np.roll(e[(r + S) % N], -1))
    k = g[5]; n = int(rng.integers(2, 18)); e = apart(rng, 2 * n); a = e[:, :n]; b = e[:, n:]
    for r in range(N):
        s = (r + S) % N
        x[r, k][:, P + a[r]] = rng.integers(0, 8, (16, n)); trig[r, k, a[r]] = P + a[r]; src[r, k, b[r]] = P + b[r]
        tg[r, k] = aimed(rng, np.concatenate([a[r], b[r] ^ 1]), P + np.concatenate([b[s], a[s]]))
    return pack(x, src, trig, tg, th)
def setup_inputs_spread(rng):
    x, src, trig, tg, th = parts(rng)
    level = rng.integers(0, 16, (N, 8, 1, W)).astype(np.float32); width = np.exp2(rng.integers(-1, 4, (N, 8, 1, W))).astype(np.float32)
    x = np.clip(np.rint(level + width * rng.standard_normal((N, 8, 16, W), dtype=np.float32)), 0, 15).astype(np.int16)
    src = np.minimum((W * rng.random((N, 8, M)) ** 3).astype(np.int64), W - 1); trig = np.minimum((W * rng.random((N, 8, M)) ** 2).astype(np.int64), W - 1)
    tg[:, 1::2] = np.sort(tg[:, 1::2], axis=-1); th = rng.integers(20, 161, (N, 8, 1))
    return pack(x, src, trig, tg, th)
def check_inputs(d):
    bad = []
    v = np.asarray(d["x"], np.float32)
    if not (np.min(v) >= 0 and np.max(v) <= 15 and np.all(v == np.floor(v))): bad.append("numbers of x")
    for k, lo, hi in (("src", 0, W - 1), ("trig", 0, W - 1), ("tg", 0, W - 1), ("th", 0, 241)):
        if np.min(d[k]) < lo or np.max(d[k]) > hi: bad.append("range of " + k)
    o = np.sort(np.stack([gentries(a) for a in d["tg"]]), axis=-1)
    if np.any(o[..., 1:] == o[..., :-1]): bad.append("targets of a rank and group differ")
    t = np.asarray(d["th"]).reshape(N, 8, 16)
    if np.any(t != t[:, :, :1]): bad.append("rows of th alike in a group")
    return bad
def reference(x, src, trig, tg, th):
    v = x.astype(np.float32).astype(np.int32).reshape(N, 8, 16, W); lim = th.astype(np.int64).reshape(N, 8, 16)[:, :, :1]
    so = np.stack([gentries(a) for a in src]).astype(np.int64); tr = np.stack([gentries(a) for a in trig]).astype(np.int64); ta = np.stack([gentries(a) for a in tg]).astype(np.int64)
    mate = np.arange(M) ^ 1
    for rnd in range(RO):
        m = v[..., P:]
        far = np.add.reduce(np.abs(np.take_along_axis(v, tr[:, :, None, :], 3) - m), axis=2)
        c = (far < lim).astype(np.int64); go = (c == 1) & (np.add.accumulate(c, axis=2) <= CAP)
        a = np.where(m >= 8, 15 - np.take_along_axis(v, so[:, :, None, :], 3), -1)
        nv = v + 0; ns = so + 0; nt = tr + 0; ng = ta + 0
        for q in range(N):
            r = (q + S) % N
            for g in range(8):
                i = np.flatnonzero(go[q, g]); b = ta[q, g, i]; col = a[q, g][:, i]
                nv[r, g][:, b] = np.where(col >= 0, col, v[r, g][:, b])
                j = b >= P; e = b[j] - P
                nt[r, g, e] = so[r, g, e]; ns[r, g, e] = so[q, g, i[j]]
                hit = np.zeros(M, bool); hit[e] = True
                ng[r, g] = np.where(hit != hit[mate], ta[r, g][mate], ta[r, g])
        v, so, tr, ta = nv, ns, nt, ng
    return {"yx": v.reshape(N, 128, W).astype(np.float32).astype(BF), "ysrc": np.stack([gtable(a) for a in so]).astype(np.float32),
            "ytrig": np.stack([gtable(a) for a in tr]).astype(np.float32), "ytg": np.stack([gtable(a) for a in ta]).astype(np.float32)}

@@ -1,0 +1,418 @@
+from concourse.bass import DstId, RemoteDMATransfer
+from concourse.mybir import AluOpType as ALU, ActivationFunctionType as ACT
+
+P, M, W, CAP, STEP, RO = 2048, 4096, 6144, 1024, 5, 3
+XW = W + CAP
+H = CAP // 2
+US = 640
+MK = 4352
+PIECES = [(0, 256, False), (256, 512, False), (512, 768, True), (768, 1024, True)]
+GCH = [(0, 768, "a"), (768, 1024, "b"), (1024, 2048, "b"), (2048, 2560, "c"), (2560, 3072, "c"),
+       (3072, 3584, "c"), (3584, 3840, "c"), (3840, 4096, "c")]
+
+SCRATCH = {}
+for _dt, _cols, _names in [
+        ("bfloat16", XW, "X"), ("bfloat16", M, "D XM"), ("float32", M, "AUX"), ("float32", XW, "U U2"),
+        ("float32", MK + 256, "WM"), ("float32", CAP, "WT GC"), ("float16", CAP, "UF"),
+        ("bfloat16", CAP, "INC GA Q A VV TT MO0 MO1 MO2 MI0 MI1 MI2"),
+        ("int32", 256, "srcI trigI tgI"), ("int32", 8, "thI pI rI"), ("float32", 8, "thF COL"), ("int32", 512, "tmpI"),
+        ("uint16", 256, "trig16"), ("uint16", 16, "mp16"), ("uint16", 64, "pi16 i16 s16 pos16 BO0 BO1 BO2 BI0 BI1 BI2"),
+        ("float32", 256, "SL LO TL CR CQ REL CW CI OS OT OG CN0 CN1 CN2"), ("bfloat16", 256, "HB AA NH CM"),
+        ("float32", 512, "PF"), ("bfloat16", 512, "PB"), ("float16", 512, "PT"), ("float32", 32, "MP CS"),
+        ("float32", 128, "KI KT FL TR BP"), ("float16", 128, "NIH"), ("float32", 384, "ZERO"),
+        ("float32", 768, "CO0 CO1 CO2"), ("bfloat16", 576, "ZB"), ("float16", 288, "ZH"), ("float32", 54, "TB"),
+        ("bfloat16", 128, "ONE BLK TRI PERM IDN I16 PSUMM PDIF")]:
+    for _n in _names.split():
+        SCRATCH[_n] = ("sbuf", [128, _cols], _dt)
+SCRATCH["RB"] = ("sbuf", [128, 257, 2], "bfloat16")
+for _b in range(8):
+    SCRATCH["B%d" % _b] = ("psum", [128, 512], "float32")
+
+NDMA = 40
+SEMAPHORES = (["sv", "ss", "sp", "sg", "sent"] + ["d%d" % k for k in range(NDMA)]
+              + ["a%s%d" % (n, r) for r in range(RO) for n in ["b", "c"] + ["m%d_" % k for k in range(len(PIECES))]])
+
+
+def helper_of(T, topo, core, dst):
+    if topo.chip(core) == topo.chip(dst):
+        return None
+    own = [c for c in topo.cores_of(core) if T.rank_of(c) is not None]
+    free = [c for c in topo.cores_of(core)
+            if T.rank_of(c) is None and topo.die(c) != topo.die(core) and topo.may_write(c, dst)]
+    if len(free) < len(own):
+        return None
+    return free[own.index(core)]
+
+
+def send(g, T, topo, src, dst, out, in_, sem):
+    rid, pid, _se = topo.addr(dst)
+    g.remote_dma(out, in_, T.sem[sem], T.sem.sent, pid, rid, topo.mask(src, dst))
+    return len(topo.engines(src, dst))
+
+
+def relay_program(g, core, T, topo):
+    n = len(T.cores)
+    for q in range(n):
+        src, dst = T.cores[q], T.cores[(q + STEP) % n]
+        if helper_of(T, topo, src, dst) != core:
+            continue
+        sent = 0
+        for r in range(RO):
+            for k, (a, b, far) in enumerate(PIECES):
+                if far:
+                    g.wait_ge(T.sem["am%d_%d" % (k, r)], len(topo.engines(src, core)))
+                    sent += send(g, T, topo, core, dst, T["MI%d" % r][:, a:b], T["MI%d" % r][:, a:b], "am%d_%d" % (k, r))
+        if sent:
+            g.wait_ge(T.sem.sent, sent)
+
+
+def rank_program(g, core, T, topo):
+    rank = T.rank_of(core)
+    if rank is None:
+        relay_program(g, core, T, topo)
+        return
+    n = len(T.cores)
+    dst = T.cores[(rank + STEP) % n]
+    frm = T.cores[(rank - STEP) % n]
+    via = helper_of(T, topo, core, dst)
+    via_in = helper_of(T, topo, frm, core)
+
+    qs = {"v": g.vector, "s": g.scalar, "p": g.tensor, "g": g, "y": g.sync}
+    known = {e: {} for e in qs}
+    count = {}
+    wrote, readers = {}, {}
+    ndma = [0]
+    nsent = [0]
+    serial = [0]
+
+    def need(e, tok):
+        sem, c, clock = tok[0], tok[1], tok[2]
+        if known[e].get(sem, 0) >= c:
+            return
+        qs[e].wait_ge(T.sem[sem], c)
+        known[e][sem] = c
+        for s, k in clock.items():
+            if known[e].get(s, 0) < k:
+                known[e][s] = k
+
+    def before(e, reads, writes):
+        toks = []
+        for x in reads:
+            if x in wrote:
+                toks.append(wrote[x])
+            if x[0] == "#":
+                toks += [t for t in readers.get(x, []) if t[3] != e]
+        for x in writes:
+            if x in wrote:
+                toks.append(wrote[x])
+            toks += readers.get(x, [])
+        toks.sort(key=lambda t: -t[4])
+        for t in toks:
+            need(e, t)
+
+    def after(e, sem, c, reads, writes):
+        serial[0] += 1
+        count[sem] = c
+        tok = (sem, c, dict(known[e]), e, serial[0])
+        for x in reads:
+            readers.setdefault(x, []).append(tok)
+        for x in writes:
+            wrote[x] = tok
+            readers[x] = []
+
+    def op(e, call, reads, writes):
+        before(e, reads, writes)
+        sem = "s" + e
+        call().then_inc(T.sem[sem], 1)
+        after(e, sem, count.get(sem, 0) + 1, reads, writes)
+
+    def dma(e, pairs, reads, writes):
+        before(e, reads, writes)
+        sem = "d%d" % ndma[0]
+        ndma[0] += 1
+        for o, i in pairs:
+            qs[e].dma_start(o, i).then_inc(T.sem[sem], 16)
+        after(e, sem, 16 * len(pairs), reads, writes)
+
+    def post(to, out, in_, sem, reads):
+        before("g", reads, [])
+        nsent[0] += send(g, T, topo, core, to, out, in_, sem)
+
+    def arrives(name, sem, sender):
+        serial[0] += 1
+        c = len(topo.engines(sender, core))
+        count[sem] = c
+        wrote[name] = (sem, c, {}, "far", serial[0])
+
+    V, S, PE = g.vector, g.scalar, g.tensor
+
+    def ts(out, in0, s1, s2, o0, o1, reads, writes):
+        if s2 is None:
+            op("v", lambda: V.tensor_scalar(out, in0, s1, None, o0), reads, writes)
+        else:
+            op("v", lambda: V.tensor_scalar(out, in0, s1, s2, o0, o1), reads, writes)
+
+    def tt(out, in0, in1, o, reads, writes):
+        op("v", lambda: V.tensor_tensor(out, in0, in1, o), reads, writes)
+
+    def cp(out, in_, reads, writes):
+        op("v", lambda: V.tensor_copy(out, in_), reads, writes)
+
+    def ms(ap, c, writes):
+        op("v", lambda: V.memset(ap, c), [], writes)
+
+    def scan(out, d0, d1, init, reads, writes):
+        op("v", lambda: V.tensor_tensor_scan(out, d0, d1, init, ALU.add, ALU.max), reads, writes)
+
+    def act(out, in_, f, reads, writes, bias=0.0, scale=1.0):
+        op("s", lambda: S.activation(out, in_, f, bias=bias, scale=scale), reads, writes)
+
+    def mm(out, lhsT, rhs, reads, writes, start=True, stop=True):
+        op("p", lambda: PE.matmul(out, lhsT, rhs, start, stop), reads, writes)
+
+    def fold(out, Z, z0, rhs, reads, writes):
+        def call():
+            ins = None
+            for j in range(16):
+                ins = PE.matmul(out, Z[:, z0 + 15 - j:z0 + 143 - j], rhs(j), j == 0, j == 15)
+            return ins
+        op("p", call, reads, writes)
+
+    def sel(out, in_, pat, cmp, fill, base, cm, reads, writes):
+        op("g", lambda: g.affine_select(out, in_, pat, cmp, fill, base, cm), reads, writes)
+
+    B = [T["B%d" % k] for k in range(8)]
+    X = T.X
+    C = T.COL
+    SP = B[5][:, 256:512]
+    DF = B[5][:, 0:256]
+    TP = B[4][:, 256:512]
+
+    dma("s", [(T.trigI[:], T.trig[:]), (T.thI[:, 0:1], T.th[:])], [], ["trigI", "thI"])
+    dma("y", [(X[:, 0:W], T.x[:])], [], ["X"])
+    dma("y", [(T.tgI[:], T.tg[:]), (T.srcI[:], T.src[:])], [], ["srcI", "tgI"])
+
+    ms(T.ONE[:], 1.0, ["ONE"])
+    ms(T.TB[:], 0.0, ["TB0", "TB1", "TB2", "TB3", "TB4", "TB5"])
+    ms(T.AUX[:, 0:1024], 0.0, ["AUX"])
+    ms(T.ZB[:], 0.0, ["ZB"])
+    op("g", lambda: g.iota(T.pI[:, 0:1], [[1, 1]], 0, 1), [], ["pI"])
+    sel(T.BLK[:], T.ONE[:], [[-16, 8], [0, 16]], ALU.is_ge, 0.0, 0, 1, ["ONE"], ["BLK"])
+    sel(T.BLK[:], T.BLK[:], [[16, 8], [0, 16]], ALU.is_ge, 0.0, 15, -1, ["BLK"], ["BLK"])
+    op("g", lambda: g.iota(T.CI[:], [[1, 256]], 0, 0, allow_small_or_imprecise_dtypes=True), [], ["CI"])
+    sel(T.TRI[:], T.BLK[:], [[1, 128]], ALU.is_ge, 0.0, 0, -1, ["BLK"], ["TRI"])
+    sel(T.TRI[:], T.TRI[:], [[0, 8], [-1, 16]], ALU.is_ge, 0.0, 14, 0, ["TRI"], ["TRI"])
+
+    def row(tab, j, val):
+        t = T.TB[:, 9 * tab:9 * tab + 8]
+        sel(t, t, [[-16, 8]], ALU.not_equal, val, -j, 1, ["TB%d" % tab], ["TB%d" % tab])
+    act(T.WT[:], T.AUX[:, 0:1024], ACT.Identity, ["AUX"], ["WT"], bias=-2048.0)
+    for k in range(1, 4):
+        act(T.AUX[:, 1024 * k:1024 * (k + 1)], T.AUX[:, 0:1024], ACT.Copy, ["AUX"], ["AUX%d" % k])
+    act(T.WM[:, 0:CAP], T.WT[:], ACT.Copy, ["WT"], ["WM"])
+    ms(T.ZERO[:], 0.0, ["ZERO"])
+    ms(X[:, W:XW], 0.0, ["Xt"])
+    ts(T.rI[:, 0:1], T.pI[:, 0:1], 15, None, ALU.bitwise_and, None, ["pI"], ["rI"])
+    ms(T.ZH[:], 0.0, ["ZH"])
+    cp(C[:, 0:1], T.rI[:, 0:1], ["rI"], ["c0"])
+    ms(T.RB[:, 0:1, :], 0.0, ["RB0"])
+    ts(C[:, 1:2], C[:, 0:1], 15.0, None, ALU.is_equal, None, ["c0"], ["c1"])
+    ms(T.CS[:], -1000000.0, ["CS"])
+    ts(C[:, 4:5], C[:, 1:2], -1.0, 1.0 / 65536.0, ALU.add, ALU.mult, ["c1"], ["c4"])
+    ts(C[:, 2:3], C[:, 1:2], 10.0, 1.0, ALU.mult, ALU.add, ["c1"], ["c2"])
+    ts(C[:, 3:4], C[:, 1:2], -2432.515625, 1024.515625, ALU.mult, ALU.add, ["c1"], ["c3"])
+    act(T.INC[:], T.WT[:], ACT.Copy, ["WT", "c4"], ["INC"], scale=C[:, 4:5])
+    cp(T.TB[:, 0:8], T.BLK[:, 0:128:16], ["BLK"], ["TB0"])
+    ts(T.TB[:, 36:44], T.BLK[:, 0:128:16], 256.0, None, ALU.mult, None, ["BLK"], ["TB4"])
+    cp(T.TB[:, 45:53], T.BLK[:, 0:128:16], ["BLK"], ["TB5"])
+    ts(C[:, 5:6], C[:, 3:4], -0.546875, None, ALU.add, None, ["c3"], ["c5"])
+    cp(T.ZB[:, 15:144:16], T.TB[:, 0:9], ["TB0", "ZB"], ["ZB"])
+    for tab, j, val in [(1, 0, 1.0), (2, 2, 1.0), (3, 2, 16.0), (4, 15, -349.0), (5, 15, 1.0 / 11.0),
+                        (1, 1, 1.0), (2, 3, 384.0), (3, 3, 1.0)]:
+        row(tab, j, val)
+    sel(T.PERM[:], T.ONE[:], [[-2, 64], [1, 2]], ALU.is_equal, 0.0, -1, 1, ["ONE"], ["PERM"])
+    sel(T.IDN[:], T.ONE[:], [[-1, 128]], ALU.is_equal, 0.0, 0, 1, ["ONE"], ["IDN"])
+    cp(T.trig16[:], T.trigI[:], ["trigI"], ["trig16"])
+    cp(T.thF[:, 0:1], T.thI[:, 0:1], ["thI"], ["thF"])
+    ts(T.TL[:], T.trigI[:], 32.0, None, ALU.add, None, ["trigI"], ["TL"])
+    ts(T.KI[:, 0:64], T.CI[:, 0:64], 16.0, C[:, 0:1], ALU.mult, ALU.add, ["CI", "c0"], ["KIa"])
+    ts(T.CW[:], T.CI[:], C[:, 2:3], C[:, 3:4], ALU.mult, ALU.add, ["CI", "c2", "c3"], ["CW"])
+    ts(T.CS[:, 1:32:2], T.KI[:, 0:16], float(MK), None, ALU.add, None, ["KIa", "CS"], ["CS"])
+    ts(T.KI[:, 64:128], T.CI[:, 0:64], 16.0, C[:, 0:1], ALU.mult, ALU.add, ["CI", "c0"], ["KIb"])
+    ts(T.KT[:, 0:64], T.KI[:, 0:64], float(W - 16384 - 192), None, ALU.add, None, ["KIa"], ["KTa"])
+    ts(T.KT[:, 64:128], T.KI[:, 0:64], float(W - 16384 - 3072), None, ALU.add, None, ["KIa"], ["KTb"])
+    cp(T.ZH[:, 15:288:16], T.TB[:, 36:54], ["TB4", "TB5", "ZH"], ["ZH"])
+    cp(T.ZB[:, 159:576:16], T.TB[:, 9:36], ["TB1", "TB2", "TB3", "ZB"], ["ZBb"])
+    tt(T.PSUMM[:], T.PERM[:], T.IDN[:], ALU.add, ["PERM", "IDN"], ["PSUMM"])
+    tt(T.PDIF[:], T.PERM[:], T.IDN[:], ALU.subtract, ["PERM", "IDN"], ["PDIF"])
+    ts(T.I16[:], T.IDN[:], 16.0, None, ALU.mult, None, ["IDN"], ["I16"])
+    ts(T.NIH[:], T.IDN[:], -1.0, None, ALU.mult, None, ["IDN"], ["NIH"])
+
+    def clear_u():
+        dma("y", [(T.U[0:128:16, 0:W], T.ZERO[:]), (T.U2[0:128:16, 0:W], T.ZERO[:])], ["ZERO"], ["U", "U2"])
+
+    auxs = ["AUX", "AUX1", "AUX2", "AUX3"]
+
+    def pair_sums(CN):
+        mm(B[2][:, 256:512], T.PSUMM[:], T.NH[:], ["PSUMM", "NH"], ["#2"])
+        mm(B[6][:], T.PDIF[:], T.PB[:], ["PDIF", "PB"], ["#6"])
+        mm(B[7][:], T.PERM[:], T.PB[:], ["PERM", "PB"], ["#7"], stop=False)
+        act(T.CQ[:], CN[:], ACT.Identity, ["CN"], ["CQ"], bias=12582912.0)
+        act(T.AA[:], B[2][:, 256:512], ACT.Abs, ["#2"], ["AA"], bias=-1.0)
+        act(T.CR[:], T.CQ[:], ACT.Identity, ["CQ"], ["CR"], bias=-12582912.0)
+
+    def amend_s():
+        tt(TP, SP, T.NH[:], ALU.mult, ["NH", "#5"], ["#4"])
+        tt(SP, TP, T.CR[:], ALU.max, ["#4", "CR"], ["#5"])
+
+    def amend_t():
+        tt(T.PT[:, 0:256], B[6][:, 0:256], T.AA[:], ALU.mult, ["#6", "AA"], ["PT0"])
+        tt(T.PT[:, 256:512], B[6][:, 256:512], T.AA[:], ALU.mult, ["#6", "AA"], ["PT1"])
+        mm(B[7][:], T.NIH[:], T.PT[:], ["NIH", "PT0", "PT1"], ["#7"], start=False)
+
+    def commence(c0, c1, far, bank):
+        t = "%d" % c0
+        ts(T.CM[:, c0:c1], far, T.thF[:, 0:1], None, ALU.is_lt, None, [bank, "thF"], ["CM" + t])
+        scan(T.RB[:, c0 + 1:c1 + 1, 1], T.CM[:, c0:c1], T.CM[:, c0:c1], T.RB[:, c0:c0 + 1, 1] if c0 else 0.0,
+             ["CM" + t] + (["RBa0"] if c0 else []), ["RBa" + t])
+        ts(T.RB[:, c0:c1, 0], T.CM[:, c0:c1], -8192.0, None, ALU.mult, None, ["CM" + t, "RB0"], ["RBb" + t])
+
+    for r in range(RO):
+        last = r == RO - 1
+        MO, MI, BO, BI, CO, CN = (T[k + str(r)] for k in ("MO", "MI", "BO", "BI", "CO", "CN"))
+        dma("y", [(T.XM[:, 2048:M], X[:, P + 2048:W])], ["X"], ["XMc"])
+        act(T.XM[:, 0:768], X[:, P:P + 768], ACT.Copy, ["X"], ["XMa"])
+        act(T.XM[:, 768:2048], X[:, P + 768:P + 2048], ACT.Copy, ["X"], ["XMb"])
+        if r == 0:
+            clear_u()
+        for k, (a, b, part) in enumerate(GCH):
+            tt(T.D[:, a:b], X[:, 0:W].indirect(T.trig16[:, a // 16:b // 16]), T.XM[:, a:b], ALU.subtract,
+               ["X", "trig16", "XM" + part], ["D%d" % k])
+            act(T.D[:, a:b], T.D[:, a:b], ACT.Abs, ["D%d" % k], ["D%d" % k])
+            if k == 1 and r > 0:
+                pair_sums(T["CN%d" % (r - 1)])
+            if b % 1024 == 0:
+                a0 = b - 1024
+                fold(B[0][:, a0 // 16:b // 16] if b < M else B[3][:, 0:64], T.ZB, 0, lambda j: T.D[:, a0 + j:b:16],
+                     ["ZB"] + ["D%d" % h for h, (u, w, _p) in enumerate(GCH) if u >= a0 and w <= b],
+                     ["#0"] if b < M else ["#3"])
+        if r == 0:
+            ts(T.tmpI[:, 0:256], T.tgI[:], 4, None, ALU.arith_shift_right, None, ["tgI"], ["tmp0"])
+            ts(T.tmpI[:, 256:512], T.tgI[:], 15, None, ALU.bitwise_and, None, ["tgI"], ["tmp1"])
+            ts(T.PF[:, 0:256], T.tmpI[:, 0:256], -192.0, None, ALU.add, None, ["tmp0"], ["PF"])
+            cp(T.PF[:, 256:512], T.tmpI[:, 256:512], ["tmp1"], ["PF1"])
+        else:
+            amend_t()
+            act(T.PF[:], B[7][:], ACT.Copy, ["#7"], ["PF", "PF1"])
+        before("y", auxs, [])
+        dma("y", [(T.AUX[2:128:16, :], T.PF[:, 0:256]), (T.AUX[3:128:16, :], T.PF[:, 256:512])], ["PF", "PF1"], ["AUXt"])
+        commence(0, 192, B[0][:, 0:192], "#0")
+        commence(192, 256, B[3][:, 0:64], "#3")
+        rb = ["RB0", "RBa0", "RBb0", "RBa192", "RBb192"]
+        mm(B[0][:, 256:512], T.TRI[:], T.CM[:], ["TRI", "CM0", "CM192"], ["#0"])
+        act(T.REL[:], B[0][:, 256:512], ACT.Copy, ["#0"], ["REL"], scale=-1.0 / 32.0)
+        fold(B[1][:, 0:32], T.ZB, 0, lambda j: T.RB[:, j:256:16, :], ["ZB"] + rb, ["#1"])
+        mm(B[3][:, 256:257], T.BLK[:], T.RB[:, 256:257, 1], ["BLK"] + rb, ["#3"])
+        if r > 0:
+            amend_s()
+        else:
+            ts(SP, T.srcI[:], 32.0, None, ALU.add, None, ["srcI"], ["#5"])
+        cp(T.HB[:], SP, ["#5"], ["HB"])
+        tt(T.LO[:], SP, T.HB[:], ALU.subtract, ["#5", "HB"], ["LO"])
+        act(T.SL[:], SP, ACT.Copy, ["#5"], ["SL"])
+        dma("y", [(T.AUX[1:128:16, :], T.LO[:]), (T.AUX[0:128:16, :], T.SL[:])], ["SL", "LO"], auxs)
+        act(T.PB[:], T.PF[:], ACT.Copy, ["PF", "PF1"], ["PB"])
+        scan(T.MP[:], T.CS[:], B[1][:, 0:32], 0.0, ["CS", "#1"], ["MP"])
+        cp(T.mp16[:], T.MP[:, 1:32:2], ["MP"], ["mp16"])
+        tt(T.WM[:, 0:MK + 256].indirect(T.mp16[:]), T.REL[:], T.CW[:], ALU.add, ["mp16", "REL", "CW"], ["WM"])
+        scan(T.UF[:], T.INC[:], T.WM[:, 0:CAP], C[:, 5:6], ["INC", "WM", "c5"], ["UF"])
+        fold(B[2][:, 0:64], T.ZH, 0, lambda j: T.UF[:, j:CAP:16], ["ZH", "UF"], ["#2"])
+        ts(T.FL[:], T.KI[:], B[3][:, 256:257], 16384.0, ALU.is_ge, ALU.mult, ["KIa", "KIb", "#3"], ["FL"])
+        fold(B[3][:, 0:64], T.ZH, 144, lambda j: T.UF[:, j:CAP:16], ["ZH", "UF"], ["#3"])
+        if not last:
+            act(T.WM[:, 0:CAP], T.WT[:], ACT.Copy, ["WT"], ["WM"])
+        tt(DF, T.TL[:], SP, ALU.subtract, ["TL"], ["#5"])
+        tt(T.TR[:], T.FL[:], T.KT[:], ALU.add, ["FL", "KTa", "KTb"], ["TR"])
+        ts(T.pi16[:], B[2][:, 0:64], -4423552.0, 4095.0, ALU.add, ALU.min, ["#2"], ["pi16"])
+        aux = auxs + ["pi16", "AUXt"]
+        cp(T.GA[:, 0:H], T.AUX[:, 0:M].indirect(T.pi16[:, 0:32]), aux, ["GA0"])
+        act(T.GA[:, H:CAP], T.AUX[:, 0:M].indirect(T.pi16[:, 32:64]), ACT.Copy, aux, ["GA1"])
+        fold(B[4][:, 0:64], T.ZB, 144, lambda j: T.GA[:, j:CAP:16], ["ZBb", "GA0", "GA1"], ["#4"])
+        fold(B[2][:, 0:64], T.ZB, 288, lambda j: T.GA[:, j:CAP:16], ["ZBb", "GA0", "GA1"], ["#2"])
+        fold(B[1][:, 0:64], T.ZB, 432, lambda j: T.GA[:, j:CAP:16], ["ZBb", "GA0", "GA1"], ["#1"])
+        ts(T.i16[:], B[3][:, 0:64], -15231.75, 4095.0, ALU.add, ALU.min, ["#3"], ["i16"])
+        act(T.Q[:, 0:H], X[:, P:W].indirect(T.i16[:, 0:32]), ACT.Relu, ["X", "i16"], ["Q0"], bias=128.0, scale=-16.0)
+        ts(T.Q[:, H:CAP], X[:, P:W].indirect(T.i16[:, 32:64]), 8.0, 16.0, ALU.is_lt, ALU.mult, ["X", "i16"], ["Q1"])
+        act(T.GC[:], T.AUX[:, 0:M].indirect(T.pi16[:]), ACT.Copy, aux, ["GC"])
+        ts(T.s16[:], B[4][:, 0:64], -32.0, None, ALU.add, None, ["#4"], ["s16"])
+        for k, (a, b, far) in enumerate(PIECES):
+            if k == 2:
+                tt(T.BP[:, 0:64], B[2][:, 0:64], T.TR[:, 0:64], ALU.max, ["#2", "TR"], ["BPa"])
+                ts(T.pos16[:], T.BP[:, 0:64], 192.0, None, ALU.add, None, ["BPa"], ["pos16"])
+            if k == 3:
+                tt(T.BP[:, 64:128], B[1][:, 0:64], T.TR[:, 64:128], ALU.max, ["#1", "TR"], ["BPb"])
+                ts(BO[:], T.BP[:, 64:128], 3072.0, None, ALU.add, None, ["BPb"], ["BO"])
+                post(dst, BI[:], BO[:], "ab%d" % r, ["BO"])
+            tt(MO[:, a:b], X[:, 0:W].indirect(T.s16[:, a // 16:b // 16]), T.Q[:, a:b], ALU.max,
+               ["X", "s16", "Q1" if a >= H else "Q0"], ["MO%d" % k])
+            post(via if (far and via is not None) else dst, MI[:, a:b], MO[:, a:b], "am%d_%d" % (k, r), ["MO%d" % k])
+        op("s", lambda: S.activation(T.U[:, 0:XW].indirect(T.pos16[:, 0:US // 16]), T.GC[:, 0:US], ACT.Silu),
+           ["pos16", "GC"], ["U"])
+        cp(T.U2[:, 0:XW].indirect(T.pos16[:, US // 16:64]), T.GC[:, US:CAP], ["pos16", "GC"], ["U2"])
+        dma("y", [(CO[:, 0:384], T.U[0:128:16, 0:W])], ["U"], ["COa"])
+        dma("y", [(CO[:, 384:768], T.U2[0:128:16, 0:W])], ["U2"], ["COb"])
+        before("g", ["COa", "COb"], [])
+        rid, pid, _se = topo.addr(dst)
+        g.remote_dma_fused([RemoteDMATransfer(dst_ids=[DstId(rid=rid, pnc=pid)], dma_engine_mask=topo.mask(core, dst),
+                                              remote_sem=T.sem["ac%d" % r], srcs=[CO[:, 128:384], CO[:, 512:768]],
+                                              dsts=[CN[:]], alu_op=1)], local_sem=T.sem.sent)
+        nsent[0] += len(topo.engines(core, dst))
+        if not last:
+            clear_u()
+        arrives("BI", "ab%d" % r, frm)
+        for k, (a, b, far) in enumerate(PIECES):
+            arrives("MI%d" % k, "am%d_%d" % (k, r), via_in if (far and via_in is not None) else frm)
+        win = X[:, 0:XW]
+        act(T.A[:, H:CAP], win.indirect(BI[:, 32:64]), ACT.Copy, ["X", "Xt", "BI"], ["AS"])
+        for k, (a, b, far) in enumerate(PIECES):
+            ix = win.indirect(BI[:, a // 16:b // 16])
+            mi = "MI%d" % k
+            if a < H:
+                if k == 0:
+                    ts(T.A[:, a:b], MI[:, a:b], 16.0, 16.0, ALU.is_ge, ALU.mult, [mi], ["A%d" % k])
+                else:
+                    act(T.A[:, a:b], MI[:, a:b], ACT.Relu, [mi], ["A%d" % k], bias=-240.0, scale=16.0)
+                act(T.VV[:, a:b], MI[:, a:b], ACT.Relu, [mi], ["VV%d" % k], bias=15.0, scale=-1.0)
+                tt(T.TT[:, a:b], ix, T.A[:, a:b], ALU.min, ["X", "Xt", "BI", "A%d" % k], ["TT%d" % k])
+            else:
+                bank = 0 if k % 2 else 3
+
+                def blend():
+                    PE.matmul(B[bank][:, 0:b - a], T.IDN[:], T.A[:, a:b], True, False)
+                    return PE.matmul(B[bank][:, 0:b - a], T.I16[:], MI[:, a:b], False, True)
+                op("p", blend, ["IDN", "I16", "AS", mi], ["#%d" % bank])
+                act(T.VV[:, a:b], MI[:, a:b], ACT.Relu, [mi], ["VV%d" % k], bias=15.0, scale=-1.0)
+                act(T.TT[:, a:b], B[bank][:, 0:b - a], ACT.Relu, ["#%d" % bank], ["TT%d" % k], bias=-256.0)
+            tt(ix, T.TT[:, a:b], T.VV[:, a:b], ALU.add, ["BI", "TT%d" % k, "VV%d" % k], ["X", "Xt"])
+        if last:
+            dma("y", [(T.yx[:], X[:, 0:W])], ["X"], ["yx"])
+        arrives("CN", "ac%d" % r, frm)
+        act(T.NH[:], CN[:], ACT.Relu, ["CN"], ["NH"], bias=1.0, scale=-1.0 / 16.0)
+        if last:
+            pair_sums(CN)
+        tt(TP, DF, T.NH[:], ALU.mult, ["#5", "NH"], ["#4"])
+        tt(T.TL[:], TP, T.SL[:], ALU.add, ["#4", "SL"], ["TL"])
+        if not last:
+            ts(T.trig16[:], T.TL[:], -32.0, None, ALU.add, None, ["TL"], ["trig16"])
+    act(T.OT[:], T.TL[:], ACT.Identity, ["TL"], ["OT"], bias=-32.0)
+    dma("s", [(T.ytrig[:], T.OT[:])], ["OT"], ["ytrig"])
+    amend_t()
+    amend_s()
+    act(T.OS[:], SP, ACT.Identity, ["#5"], ["OS"], bias=-32.0)
+    dma("s", [(T.ysrc[:], T.OS[:])], ["OS"], ["ysrc"])
+    ts(T.CQ[:], B[7][:, 0:256], 16.0, 3072.0, ALU.mult, ALU.add, ["#7"], ["CQ"])
+    tt(T.OG[:], B[7][:, 256:512], T.CQ[:], ALU.add, ["#7", "CQ"], ["OG"])
+    dma("s", [(T.ytg[:], T.OG[:])], ["OG"], ["ytg"])
+    for sem, c in count.items():
+        need("g", (sem, c, {}))
+    g.wait_ge(T.sem.sent, nsent[0])

@@ -7,8 +7,10 @@ H = CAP // 2
 US = 640
 MK = 4352
 PIECES = [(0, 256, False), (256, 512, False), (512, 768, True), (768, 1024, True)]
-GCH = [(0, 768, "a"), (768, 1024, "b"), (1024, 2048, "b"), (2048, 2560, "c"), (2560, 3072, "c"),
-       (3072, 3584, "c"), (3584, 3840, "c"), (3840, 4096, "c")]
+SEND = [0, 2, 3, 1]
+GCH = [(0, 640, "a"), (640, 1024, "a"), (3072, 3328, "b"), (1024, 1536, "c"), (1536, 2048, "c"), (2048, 2560, "d"),
+       (2560, 2816, "d"), (2816, 3072, "d")]
+ZC = 3328
 
 SCRATCH = {}
 for _dt, _cols, _names in [
@@ -21,14 +23,14 @@ for _dt, _cols, _names in [
         ("float32", 512, "PF"), ("bfloat16", 512, "PB"), ("float16", 512, "PT"), ("float32", 32, "MP CS"),
         ("float32", 128, "KI KT FL TR BP"), ("float16", 128, "NIH"), ("float32", 384, "ZERO"),
         ("float32", 768, "CO0 CO1 CO2"), ("bfloat16", 576, "ZB"), ("float16", 288, "ZH"), ("float32", 54, "TB"),
-        ("bfloat16", 128, "ONE BLK TRI PERM IDN I16 PSUMM PDIF")]:
+        ("bfloat16", 128, "ONE BLK TRI PERM IDN NIB I16 PSUMM PDIF")]:
     for _n in _names.split():
         SCRATCH[_n] = ("sbuf", [128, _cols], _dt)
 SCRATCH["RB"] = ("sbuf", [128, 257, 2], "bfloat16")
 for _b in range(8):
     SCRATCH["B%d" % _b] = ("psum", [128, 512], "float32")
 
-NDMA = 40
+NDMA = 44
 SEMAPHORES = (["sv", "ss", "sp", "sg", "sent"] + ["d%d" % k for k in range(NDMA)]
               + ["a%s%d" % (n, r) for r in range(RO) for n in ["b", "c"] + ["m%d_" % k for k in range(len(PIECES))]])
 
@@ -170,6 +172,12 @@ def rank_program(g, core, T, topo):
     def mm(out, lhsT, rhs, reads, writes, start=True, stop=True):
         op("p", lambda: PE.matmul(out, lhsT, rhs, start, stop), reads, writes)
 
+    def mm2(out, l0, r0, l1, r1, reads, writes):
+        def call():
+            PE.matmul(out, l0, r0, True, False)
+            return PE.matmul(out, l1, r1, False, True)
+        op("p", call, reads, writes)
+
     def fold(out, Z, z0, rhs, reads, writes):
         def call():
             ins = None
@@ -189,7 +197,8 @@ def rank_program(g, core, T, topo):
     TP = B[4][:, 256:512]
 
     dma("s", [(T.trigI[:], T.trig[:]), (T.thI[:, 0:1], T.th[:])], [], ["trigI", "thI"])
-    dma("y", [(X[:, 0:W], T.x[:])], [], ["X"])
+    dma("y", [(X[:, P:W], T.x[:, P:W])], [], ["Xm"])
+    dma("y", [(X[:, 0:P], T.x[:, 0:P])], [], ["X"])
     dma("y", [(T.tgI[:], T.tg[:]), (T.srcI[:], T.src[:])], [], ["srcI", "tgI"])
 
     ms(T.ONE[:], 1.0, ["ONE"])
@@ -243,73 +252,88 @@ def rank_program(g, core, T, topo):
     ts(T.KT[:, 64:128], T.KI[:, 0:64], float(W - 16384 - 3072), None, ALU.add, None, ["KIa"], ["KTb"])
     cp(T.ZH[:, 15:288:16], T.TB[:, 36:54], ["TB4", "TB5", "ZH"], ["ZH"])
     cp(T.ZB[:, 159:576:16], T.TB[:, 9:36], ["TB1", "TB2", "TB3", "ZB"], ["ZBb"])
+    ts(T.NIB[:], T.IDN[:], -1.0, None, ALU.mult, None, ["IDN"], ["NIB"])
+    ts(T.NIH[:], T.IDN[:], -1.0, None, ALU.mult, None, ["IDN"], ["NIH"])
+    ts(T.I16[:], T.IDN[:], 16.0, None, ALU.mult, None, ["IDN"], ["I16"])
     tt(T.PSUMM[:], T.PERM[:], T.IDN[:], ALU.add, ["PERM", "IDN"], ["PSUMM"])
     tt(T.PDIF[:], T.PERM[:], T.IDN[:], ALU.subtract, ["PERM", "IDN"], ["PDIF"])
-    ts(T.I16[:], T.IDN[:], 16.0, None, ALU.mult, None, ["IDN"], ["I16"])
-    ts(T.NIH[:], T.IDN[:], -1.0, None, ALU.mult, None, ["IDN"], ["NIH"])
 
     def clear_u():
         dma("y", [(T.U[0:128:16, 0:W], T.ZERO[:]), (T.U2[0:128:16, 0:W], T.ZERO[:])], ["ZERO"], ["U", "U2"])
 
     auxs = ["AUX", "AUX1", "AUX2", "AUX3"]
 
-    def pair_sums(CN):
+    def pair_sums():
         mm(B[2][:, 256:512], T.PSUMM[:], T.NH[:], ["PSUMM", "NH"], ["#2"])
         mm(B[6][:], T.PDIF[:], T.PB[:], ["PDIF", "PB"], ["#6"])
         mm(B[7][:], T.PERM[:], T.PB[:], ["PERM", "PB"], ["#7"], stop=False)
-        act(T.CQ[:], CN[:], ACT.Identity, ["CN"], ["CQ"], bias=12582912.0)
         act(T.AA[:], B[2][:, 256:512], ACT.Abs, ["#2"], ["AA"], bias=-1.0)
-        act(T.CR[:], T.CQ[:], ACT.Identity, ["CQ"], ["CR"], bias=-12582912.0)
 
-    def amend_s():
-        tt(TP, SP, T.NH[:], ALU.mult, ["NH", "#5"], ["#4"])
-        tt(SP, TP, T.CR[:], ALU.max, ["#4", "CR"], ["#5"])
+    def rounded(CN):
+        act(T.CQ[:], CN[:], ACT.Identity, ["CN"], ["CQ"], bias=12582912.0)
+        act(T.CR[:], T.CQ[:], ACT.Identity, ["CQ"], ["CR"], bias=-12582912.0)
 
     def amend_t():
         tt(T.PT[:, 0:256], B[6][:, 0:256], T.AA[:], ALU.mult, ["#6", "AA"], ["PT0"])
         tt(T.PT[:, 256:512], B[6][:, 256:512], T.AA[:], ALU.mult, ["#6", "AA"], ["PT1"])
         mm(B[7][:], T.NIH[:], T.PT[:], ["NIH", "PT0", "PT1"], ["#7"], start=False)
+        tt(TP, SP, T.NH[:], ALU.mult, ["NH", "#5"], ["#4"])
 
-    def commence(c0, c1, far, bank):
-        t = "%d" % c0
-        ts(T.CM[:, c0:c1], far, T.thF[:, 0:1], None, ALU.is_lt, None, [bank, "thF"], ["CM" + t])
-        scan(T.RB[:, c0 + 1:c1 + 1, 1], T.CM[:, c0:c1], T.CM[:, c0:c1], T.RB[:, c0:c0 + 1, 1] if c0 else 0.0,
-             ["CM" + t] + (["RBa0"] if c0 else []), ["RBa" + t])
-        ts(T.RB[:, c0:c1, 0], T.CM[:, c0:c1], -8192.0, None, ALU.mult, None, ["CM" + t, "RB0"], ["RBb" + t])
+    def amend_s():
+        tt(SP, TP, T.CR[:], ALU.max, ["#4", "CR"], ["#5"])
+
+    def flags(c0, c1, far, bank):
+        ts(T.CM[:, c0:c1], far, T.thF[:, 0:1], None, ALU.is_lt, None, [bank, "thF"], ["CM%d" % c0])
+        ts(T.RB[:, c0:c1, 0], far, T.thF[:, 0:1], -8192.0, ALU.is_lt, ALU.mult, [bank, "thF", "RB0"], ["RBb%d" % c0])
 
     for r in range(RO):
         last = r == RO - 1
         MO, MI, BO, BI, CO, CN = (T[k + str(r)] for k in ("MO", "MI", "BO", "BI", "CO", "CN"))
-        dma("y", [(T.XM[:, 2048:M], X[:, P + 2048:W])], ["X"], ["XMc"])
-        act(T.XM[:, 0:768], X[:, P:P + 768], ACT.Copy, ["X"], ["XMa"])
-        act(T.XM[:, 768:2048], X[:, P + 768:P + 2048], ACT.Copy, ["X"], ["XMb"])
+        xm = ["Xm"] if r == 0 else ["X"]
+        dma("y", [(T.XM[:, 1024:2048], X[:, P + 1024:P + 2048])], xm, ["XMc"])
+        dma("y", [(T.XM[:, 2048:3072], X[:, P + 2048:P + 3072])], xm, ["XMd"])
+        act(T.XM[:, 0:1024], X[:, P:P + 1024], ACT.Copy, xm, ["XMa"])
+        cp(T.XM[:, 3072:ZC], X[:, P + 3072:P + ZC], xm, ["XMb"])
+        act(T.XM[:, ZC:M], X[:, 0:W].indirect(T.trig16[:, ZC // 16:256]), ACT.Copy, ["X", "Xm", "trig16"], ["XMz"])
+        if r > 0:
+            pair_sums()
+        zs = [(ZC, ZC + 512, B[1][:], "#1"), (ZC + 512, M, B[4][:, 0:256], "#4")]
+        for a, b, ps, bank in zs:
+            mm2(ps, T.IDN[:], T.XM[:, a:b], T.NIB[:], X[:, P + a:P + b], ["IDN", "NIB", "XMz", "X", "Xm"], [bank])
         if r == 0:
             clear_u()
         for k, (a, b, part) in enumerate(GCH):
             tt(T.D[:, a:b], X[:, 0:W].indirect(T.trig16[:, a // 16:b // 16]), T.XM[:, a:b], ALU.subtract,
-               ["X", "trig16", "XM" + part], ["D%d" % k])
+               ["X", "Xm", "trig16", "XM" + part], ["D%d" % k])
             act(T.D[:, a:b], T.D[:, a:b], ACT.Abs, ["D%d" % k], ["D%d" % k])
-            if k == 1 and r > 0:
-                pair_sums(T["CN%d" % (r - 1)])
-            if b % 1024 == 0:
+            if k == 1:
+                for u, w, ps, bank in zs:
+                    act(T.D[:, u:w], ps, ACT.Abs, [bank], ["Dz" + bank])
+            if b % 1024 == 0 or b == ZC:
+                b = M if b == ZC else b
                 a0 = b - 1024
-                fold(B[0][:, a0 // 16:b // 16] if b < M else B[3][:, 0:64], T.ZB, 0, lambda j: T.D[:, a0 + j:b:16],
-                     ["ZB"] + ["D%d" % h for h, (u, w, _p) in enumerate(GCH) if u >= a0 and w <= b],
-                     ["#0"] if b < M else ["#3"])
+                fold(B[3][:, 0:64] if b == 3072 else B[0][:, a0 // 16:b // 16], T.ZB, 0, lambda j: T.D[:, a0 + j:b:16],
+                     ["ZB"] + (["Dz#1", "Dz#4"] if b == M else [])
+                     + ["D%d" % h for h, (u, w, _p) in enumerate(GCH) if u >= a0 and w <= b],
+                     ["#3"] if b == 3072 else ["#0"])
         if r == 0:
             ts(T.tmpI[:, 0:256], T.tgI[:], 4, None, ALU.arith_shift_right, None, ["tgI"], ["tmp0"])
             ts(T.tmpI[:, 256:512], T.tgI[:], 15, None, ALU.bitwise_and, None, ["tgI"], ["tmp1"])
             ts(T.PF[:, 0:256], T.tmpI[:, 0:256], -192.0, None, ALU.add, None, ["tmp0"], ["PF"])
             cp(T.PF[:, 256:512], T.tmpI[:, 256:512], ["tmp1"], ["PF1"])
         else:
+            rounded(T["CN%d" % (r - 1)])
             amend_t()
             act(T.PF[:], B[7][:], ACT.Copy, ["#7"], ["PF", "PF1"])
         before("y", auxs, [])
         dma("y", [(T.AUX[2:128:16, :], T.PF[:, 0:256]), (T.AUX[3:128:16, :], T.PF[:, 256:512])], ["PF", "PF1"], ["AUXt"])
-        commence(0, 192, B[0][:, 0:192], "#0")
-        commence(192, 256, B[3][:, 0:64], "#3")
-        rb = ["RB0", "RBa0", "RBb0", "RBa192", "RBb192"]
-        mm(B[0][:, 256:512], T.TRI[:], T.CM[:], ["TRI", "CM0", "CM192"], ["#0"])
+        flags(0, 128, B[0][:, 0:128], "#0")
+        flags(192, 256, B[0][:, 192:256], "#0")
+        scan(T.RB[:, 1:129, 1], T.CM[:, 0:128], T.CM[:, 0:128], 0.0, ["CM0"], ["RBa0"])
+        flags(128, 192, B[3][:, 0:64], "#3")
+        scan(T.RB[:, 129:257, 1], T.CM[:, 128:256], T.CM[:, 128:256], T.RB[:, 128:129, 1], ["CM128", "CM192", "RBa0"], ["RBa1"])
+        rb = ["RB0", "RBa0", "RBa1", "RBb0", "RBb128", "RBb192"]
+        mm(B[0][:, 256:512], T.TRI[:], T.CM[:], ["TRI", "CM0", "CM128", "CM192"], ["#0"])
         act(T.REL[:], B[0][:, 256:512], ACT.Copy, ["#0"], ["REL"], scale=-1.0 / 32.0)
         fold(B[1][:, 0:32], T.ZB, 0, lambda j: T.RB[:, j:256:16, :], ["ZB"] + rb, ["#1"])
         mm(B[3][:, 256:257], T.BLK[:], T.RB[:, 256:257, 1], ["BLK"] + rb, ["#3"])
@@ -345,11 +369,12 @@ def rank_program(g, core, T, topo):
         ts(T.Q[:, H:CAP], X[:, P:W].indirect(T.i16[:, 32:64]), 8.0, 16.0, ALU.is_lt, ALU.mult, ["X", "i16"], ["Q1"])
         act(T.GC[:], T.AUX[:, 0:M].indirect(T.pi16[:]), ACT.Copy, aux, ["GC"])
         ts(T.s16[:], B[4][:, 0:64], -32.0, None, ALU.add, None, ["#4"], ["s16"])
-        for k, (a, b, far) in enumerate(PIECES):
-            if k == 2:
+        for step, k in enumerate(SEND):
+            a, b, far = PIECES[k]
+            if step == 2:
                 tt(T.BP[:, 0:64], B[2][:, 0:64], T.TR[:, 0:64], ALU.max, ["#2", "TR"], ["BPa"])
                 ts(T.pos16[:], T.BP[:, 0:64], 192.0, None, ALU.add, None, ["BPa"], ["pos16"])
-            if k == 3:
+            if step == 3:
                 tt(T.BP[:, 64:128], B[1][:, 0:64], T.TR[:, 64:128], ALU.max, ["#1", "TR"], ["BPb"])
                 ts(BO[:], T.BP[:, 64:128], 3072.0, None, ALU.add, None, ["BPb"], ["BO"])
                 post(dst, BI[:], BO[:], "ab%d" % r, ["BO"])
@@ -386,11 +411,7 @@ def rank_program(g, core, T, topo):
                 tt(T.TT[:, a:b], ix, T.A[:, a:b], ALU.min, ["X", "Xt", "BI", "A%d" % k], ["TT%d" % k])
             else:
                 bank = 0 if k % 2 else 3
-
-                def blend():
-                    PE.matmul(B[bank][:, 0:b - a], T.IDN[:], T.A[:, a:b], True, False)
-                    return PE.matmul(B[bank][:, 0:b - a], T.I16[:], MI[:, a:b], False, True)
-                op("p", blend, ["IDN", "I16", "AS", mi], ["#%d" % bank])
+                mm2(B[bank][:, 0:b - a], T.IDN[:], T.A[:, a:b], T.I16[:], MI[:, a:b], ["IDN", "I16", "AS", mi], ["#%d" % bank])
                 act(T.VV[:, a:b], MI[:, a:b], ACT.Relu, [mi], ["VV%d" % k], bias=15.0, scale=-1.0)
                 act(T.TT[:, a:b], B[bank][:, 0:b - a], ACT.Relu, ["#%d" % bank], ["TT%d" % k], bias=-256.0)
             tt(ix, T.TT[:, a:b], T.VV[:, a:b], ALU.add, ["BI", "TT%d" % k, "VV%d" % k], ["X", "Xt"])
@@ -399,7 +420,8 @@ def rank_program(g, core, T, topo):
         arrives("CN", "ac%d" % r, frm)
         act(T.NH[:], CN[:], ACT.Relu, ["CN"], ["NH"], bias=1.0, scale=-1.0 / 16.0)
         if last:
-            pair_sums(CN)
+            pair_sums()
+            rounded(CN)
         tt(TP, DF, T.NH[:], ALU.mult, ["#5", "NH"], ["#4"])
         tt(T.TL[:], TP, T.SL[:], ALU.add, ["#4", "SL"], ["TL"])
         if not last:

from concourse.bass import DstId, RemoteDMATransfer
from concourse.mybir import AluOpType as ALU, ActivationFunctionType as ACT

P, M, W, CAP, STEP, RO = 2048, 4096, 6144, 1024, 5, 3
XW = W + CAP
H = CAP // 2
US = 640
MK = 4352
PIECES = [(0, 256, False), (256, 512, False), (512, 768, True), (768, 1024, True)]
SEND = [0, 2, 3, 1]
GCH = [(0, 640, "a"), (640, 1024, "a"), (3072, 3328, "b"), (1024, 1536, "c"), (1536, 2048, "c"), (2048, 2560, "d"),
       (2560, 2816, "d"), (2816, 3072, "d")]
ZC = 3328

SCRATCH = {}
for _dt, _cols, _names in [
        ("bfloat16", XW, "X"), ("bfloat16", M, "D XM"), ("float32", M, "AUX"), ("float32", XW, "U U2"),
        ("float32", MK + 256, "WM"), ("float32", CAP, "WT GC"), ("float16", CAP, "UF"),
        ("bfloat16", CAP, "INC GA Q A VV TT MO0 MO1 MO2 MI0 MI1 MI2"),
        ("int32", 256, "srcI trigI tgI"), ("int32", 8, "thI pI rI"), ("float32", 8, "thF COL"), ("int32", 512, "tmpI"),
        ("uint16", 256, "trig16"), ("uint16", 16, "mp16"), ("uint16", 64, "pi16 i16 s16 pos16 BO0 BO1 BO2 BI0 BI1 BI2"),
        ("float32", 256, "SL LO TL CR CQ REL CW CI OS OT OG CN0 CN1 CN2"), ("bfloat16", 256, "HB AA NH CM"),
        ("float32", 512, "PF"), ("bfloat16", 512, "PB"), ("float16", 512, "PT"), ("float32", 32, "MP CS"),
        ("float32", 128, "KI KT FL TR BP"), ("float16", 128, "NIH"), ("float32", 384, "ZERO"),
        ("float32", 768, "CO0 CO1 CO2"), ("bfloat16", 576, "ZB"), ("float16", 288, "ZH"), ("float32", 54, "TB"),
        ("bfloat16", 128, "ONE BLK TRI PERM IDN NIB I16 PSUMM PDIF")]:
    for _n in _names.split():
        SCRATCH[_n] = ("sbuf", [128, _cols], _dt)
SCRATCH["RB"] = ("sbuf", [128, 257, 2], "bfloat16")
for _b in range(8):
    SCRATCH["B%d" % _b] = ("psum", [128, 512], "float32")

NDMA = 44
SEMAPHORES = (["sv", "ss", "sp", "sg", "sent"] + ["d%d" % k for k in range(NDMA)]
              + ["a%s%d" % (n, r) for r in range(RO) for n in ["b", "c"] + ["m%d_" % k for k in range(len(PIECES))]])


def helper_of(T, topo, core, dst):
    if topo.chip(core) == topo.chip(dst):
        return None
    own = [c for c in topo.cores_of(core) if T.rank_of(c) is not None]
    free = [c for c in topo.cores_of(core)
            if T.rank_of(c) is None and topo.die(c) != topo.die(core) and topo.may_write(c, dst)]
    if len(free) < len(own):
        return None
    return free[own.index(core)]


def send(g, T, topo, src, dst, out, in_, sem):
    rid, pid, _se = topo.addr(dst)
    g.remote_dma(out, in_, T.sem[sem], T.sem.sent, pid, rid, topo.mask(src, dst))
    return len(topo.engines(src, dst))


def relay_program(g, core, T, topo):
    n = len(T.cores)
    for q in range(n):
        src, dst = T.cores[q], T.cores[(q + STEP) % n]
        if helper_of(T, topo, src, dst) != core:
            continue
        sent = 0
        for r in range(RO):
            for k, (a, b, far) in enumerate(PIECES):
                if far:
                    g.wait_ge(T.sem["am%d_%d" % (k, r)], len(topo.engines(src, core)))
                    sent += send(g, T, topo, core, dst, T["MI%d" % r][:, a:b], T["MI%d" % r][:, a:b], "am%d_%d" % (k, r))
        if sent:
            g.wait_ge(T.sem.sent, sent)


def rank_program(g, core, T, topo):
    rank = T.rank_of(core)
    if rank is None:
        relay_program(g, core, T, topo)
        return
    n = len(T.cores)
    dst = T.cores[(rank + STEP) % n]
    frm = T.cores[(rank - STEP) % n]
    via = helper_of(T, topo, core, dst)
    via_in = helper_of(T, topo, frm, core)

    qs = {"v": g.vector, "s": g.scalar, "p": g.tensor, "g": g, "y": g.sync}
    known = {e: {} for e in qs}
    count = {}
    wrote, readers = {}, {}
    ndma = [0]
    nsent = [0]
    serial = [0]

    def need(e, tok):
        sem, c, clock = tok[0], tok[1], tok[2]
        if known[e].get(sem, 0) >= c:
            return
        qs[e].wait_ge(T.sem[sem], c)
        known[e][sem] = c
        for s, k in clock.items():
            if known[e].get(s, 0) < k:
                known[e][s] = k

    def before(e, reads, writes):
        toks = []
        for x in reads:
            if x in wrote:
                toks.append(wrote[x])
            if x[0] == "#":
                toks += [t for t in readers.get(x, []) if t[3] != e]
        for x in writes:
            if x in wrote:
                toks.append(wrote[x])
            toks += readers.get(x, [])
        toks.sort(key=lambda t: -t[4])
        for t in toks:
            need(e, t)

    def after(e, sem, c, reads, writes):
        serial[0] += 1
        count[sem] = c
        tok = (sem, c, dict(known[e]), e, serial[0])
        for x in reads:
            readers.setdefault(x, []).append(tok)
        for x in writes:
            wrote[x] = tok
            readers[x] = []

    def op(e, call, reads, writes):
        before(e, reads, writes)
        sem = "s" + e
        call().then_inc(T.sem[sem], 1)
        after(e, sem, count.get(sem, 0) + 1, reads, writes)

    def dma(e, pairs, reads, writes):
        before(e, reads, writes)
        sem = "d%d" % ndma[0]
        ndma[0] += 1
        for o, i in pairs:
            qs[e].dma_start(o, i).then_inc(T.sem[sem], 16)
        after(e, sem, 16 * len(pairs), reads, writes)

    def post(to, out, in_, sem, reads):
        before("g", reads, [])
        nsent[0] += send(g, T, topo, core, to, out, in_, sem)

    def arrives(name, sem, sender):
        serial[0] += 1
        c = len(topo.engines(sender, core))
        count[sem] = c
        wrote[name] = (sem, c, {}, "far", serial[0])

    V, S, PE = g.vector, g.scalar, g.tensor

    def ts(out, in0, s1, s2, o0, o1, reads, writes):
        if s2 is None:
            op("v", lambda: V.tensor_scalar(out, in0, s1, None, o0), reads, writes)
        else:
            op("v", lambda: V.tensor_scalar(out, in0, s1, s2, o0, o1), reads, writes)

    def tt(out, in0, in1, o, reads, writes):
        op("v", lambda: V.tensor_tensor(out, in0, in1, o), reads, writes)

    def cp(out, in_, reads, writes):
        op("v", lambda: V.tensor_copy(out, in_), reads, writes)

    def ms(ap, c, writes):
        op("v", lambda: V.memset(ap, c), [], writes)

    def scan(out, d0, d1, init, reads, writes):
        op("v", lambda: V.tensor_tensor_scan(out, d0, d1, init, ALU.add, ALU.max), reads, writes)

    def act(out, in_, f, reads, writes, bias=0.0, scale=1.0):
        op("s", lambda: S.activation(out, in_, f, bias=bias, scale=scale), reads, writes)

    def mm(out, lhsT, rhs, reads, writes, start=True, stop=True):
        op("p", lambda: PE.matmul(out, lhsT, rhs, start, stop), reads, writes)

    def mm2(out, l0, r0, l1, r1, reads, writes):
        def call():
            PE.matmul(out, l0, r0, True, False)
            return PE.matmul(out, l1, r1, False, True)
        op("p", call, reads, writes)

    def fold(out, Z, z0, rhs, reads, writes):
        def call():
            ins = None
            for j in range(16):
                ins = PE.matmul(out, Z[:, z0 + 15 - j:z0 + 143 - j], rhs(j), j == 0, j == 15)
            return ins
        op("p", call, reads, writes)

    def sel(out, in_, pat, cmp, fill, base, cm, reads, writes):
        op("g", lambda: g.affine_select(out, in_, pat, cmp, fill, base, cm), reads, writes)

    B = [T["B%d" % k] for k in range(8)]
    X = T.X
    C = T.COL
    SP = B[5][:, 256:512]
    DF = B[5][:, 0:256]
    TP = B[4][:, 256:512]

    dma("s", [(T.trigI[:], T.trig[:]), (T.thI[:, 0:1], T.th[:])], [], ["trigI", "thI"])
    dma("y", [(X[:, P:W], T.x[:, P:W])], [], ["Xm"])
    dma("y", [(X[:, 0:P], T.x[:, 0:P])], [], ["X"])
    dma("y", [(T.tgI[:], T.tg[:]), (T.srcI[:], T.src[:])], [], ["srcI", "tgI"])

    ms(T.ONE[:], 1.0, ["ONE"])
    ms(T.TB[:], 0.0, ["TB0", "TB1", "TB2", "TB3", "TB4", "TB5"])
    ms(T.AUX[:, 0:1024], 0.0, ["AUX"])
    ms(T.ZB[:], 0.0, ["ZB"])
    op("g", lambda: g.iota(T.pI[:, 0:1], [[1, 1]], 0, 1), [], ["pI"])
    sel(T.BLK[:], T.ONE[:], [[-16, 8], [0, 16]], ALU.is_ge, 0.0, 0, 1, ["ONE"], ["BLK"])
    sel(T.BLK[:], T.BLK[:], [[16, 8], [0, 16]], ALU.is_ge, 0.0, 15, -1, ["BLK"], ["BLK"])
    op("g", lambda: g.iota(T.CI[:], [[1, 256]], 0, 0, allow_small_or_imprecise_dtypes=True), [], ["CI"])
    sel(T.TRI[:], T.BLK[:], [[1, 128]], ALU.is_ge, 0.0, 0, -1, ["BLK"], ["TRI"])
    sel(T.TRI[:], T.TRI[:], [[0, 8], [-1, 16]], ALU.is_ge, 0.0, 14, 0, ["TRI"], ["TRI"])

    def row(tab, j, val):
        t = T.TB[:, 9 * tab:9 * tab + 8]
        sel(t, t, [[-16, 8]], ALU.not_equal, val, -j, 1, ["TB%d" % tab], ["TB%d" % tab])
    act(T.WT[:], T.AUX[:, 0:1024], ACT.Identity, ["AUX"], ["WT"], bias=-2048.0)
    for k in range(1, 4):
        act(T.AUX[:, 1024 * k:1024 * (k + 1)], T.AUX[:, 0:1024], ACT.Copy, ["AUX"], ["AUX%d" % k])
    act(T.WM[:, 0:CAP], T.WT[:], ACT.Copy, ["WT"], ["WM"])
    ms(T.ZERO[:], 0.0, ["ZERO"])
    ms(X[:, W:XW], 0.0, ["Xt"])
    ts(T.rI[:, 0:1], T.pI[:, 0:1], 15, None, ALU.bitwise_and, None, ["pI"], ["rI"])
    ms(T.ZH[:], 0.0, ["ZH"])
    cp(C[:, 0:1], T.rI[:, 0:1], ["rI"], ["c0"])
    ms(T.RB[:, 0:1, :], 0.0, ["RB0"])
    ts(C[:, 1:2], C[:, 0:1], 15.0, None, ALU.is_equal, None, ["c0"], ["c1"])
    ms(T.CS[:], -1000000.0, ["CS"])
    ts(C[:, 4:5], C[:, 1:2], -1.0, 1.0 / 65536.0, ALU.add, ALU.mult, ["c1"], ["c4"])
    ts(C[:, 2:3], C[:, 1:2], 10.0, 1.0, ALU.mult, ALU.add, ["c1"], ["c2"])
    ts(C[:, 3:4], C[:, 1:2], -2432.515625, 1024.515625, ALU.mult, ALU.add, ["c1"], ["c3"])
    act(T.INC[:], T.WT[:], ACT.Copy, ["WT", "c4"], ["INC"], scale=C[:, 4:5])
    cp(T.TB[:, 0:8], T.BLK[:, 0:128:16], ["BLK"], ["TB0"])
    ts(T.TB[:, 36:44], T.BLK[:, 0:128:16], 256.0, None, ALU.mult, None, ["BLK"], ["TB4"])
    cp(T.TB[:, 45:53], T.BLK[:, 0:128:16], ["BLK"], ["TB5"])
    ts(C[:, 5:6], C[:, 3:4], -0.546875, None, ALU.add, None, ["c3"], ["c5"])
    cp(T.ZB[:, 15:144:16], T.TB[:, 0:9], ["TB0", "ZB"], ["ZB"])
    for tab, j, val in [(1, 0, 1.0), (2, 2, 1.0), (3, 2, 16.0), (4, 15, -349.0), (5, 15, 1.0 / 11.0),
                        (1, 1, 1.0), (2, 3, 384.0), (3, 3, 1.0)]:
        row(tab, j, val)
    sel(T.PERM[:], T.ONE[:], [[-2, 64], [1, 2]], ALU.is_equal, 0.0, -1, 1, ["ONE"], ["PERM"])
    sel(T.IDN[:], T.ONE[:], [[-1, 128]], ALU.is_equal, 0.0, 0, 1, ["ONE"], ["IDN"])
    cp(T.trig16[:], T.trigI[:], ["trigI"], ["trig16"])
    cp(T.thF[:, 0:1], T.thI[:, 0:1], ["thI"], ["thF"])
    ts(T.TL[:], T.trigI[:], 32.0, None, ALU.add, None, ["trigI"], ["TL"])
    ts(T.KI[:, 0:64], T.CI[:, 0:64], 16.0, C[:, 0:1], ALU.mult, ALU.add, ["CI", "c0"], ["KIa"])
    ts(T.CW[:], T.CI[:], C[:, 2:3], C[:, 3:4], ALU.mult, ALU.add, ["CI", "c2", "c3"], ["CW"])
    ts(T.CS[:, 1:32:2], T.KI[:, 0:16], float(MK), None, ALU.add, None, ["KIa", "CS"], ["CS"])
    ts(T.KI[:, 64:128], T.CI[:, 0:64], 16.0, C[:, 0:1], ALU.mult, ALU.add, ["CI", "c0"], ["KIb"])
    ts(T.KT[:, 0:64], T.KI[:, 0:64], float(W - 16384 - 192), None, ALU.add, None, ["KIa"], ["KTa"])
    ts(T.KT[:, 64:128], T.KI[:, 0:64], float(W - 16384 - 3072), None, ALU.add, None, ["KIa"], ["KTb"])
    cp(T.ZH[:, 15:288:16], T.TB[:, 36:54], ["TB4", "TB5", "ZH"], ["ZH"])
    cp(T.ZB[:, 159:576:16], T.TB[:, 9:36], ["TB1", "TB2", "TB3", "ZB"], ["ZBb"])
    ts(T.NIB[:], T.IDN[:], -1.0, None, ALU.mult, None, ["IDN"], ["NIB"])
    ts(T.NIH[:], T.IDN[:], -1.0, None, ALU.mult, None, ["IDN"], ["NIH"])
    ts(T.I16[:], T.IDN[:], 16.0, None, ALU.mult, None, ["IDN"], ["I16"])
    tt(T.PSUMM[:], T.PERM[:], T.IDN[:], ALU.add, ["PERM", "IDN"], ["PSUMM"])
    tt(T.PDIF[:], T.PERM[:], T.IDN[:], ALU.subtract, ["PERM", "IDN"], ["PDIF"])

    def clear_u():
        dma("y", [(T.U[0:128:16, 0:W], T.ZERO[:]), (T.U2[0:128:16, 0:W], T.ZERO[:])], ["ZERO"], ["U", "U2"])

    auxs = ["AUX", "AUX1", "AUX2", "AUX3"]

    def pair_sums():
        mm(B[2][:, 256:512], T.PSUMM[:], T.NH[:], ["PSUMM", "NH"], ["#2"])
        mm(B[6][:], T.PDIF[:], T.PB[:], ["PDIF", "PB"], ["#6"])
        mm(B[7][:], T.PERM[:], T.PB[:], ["PERM", "PB"], ["#7"], stop=False)
        act(T.AA[:], B[2][:, 256:512], ACT.Abs, ["#2"], ["AA"], bias=-1.0)

    def rounded(CN):
        act(T.CQ[:], CN[:], ACT.Identity, ["CN"], ["CQ"], bias=12582912.0)
        act(T.CR[:], T.CQ[:], ACT.Identity, ["CQ"], ["CR"], bias=-12582912.0)

    def amend_t():
        tt(T.PT[:, 0:256], B[6][:, 0:256], T.AA[:], ALU.mult, ["#6", "AA"], ["PT0"])
        tt(T.PT[:, 256:512], B[6][:, 256:512], T.AA[:], ALU.mult, ["#6", "AA"], ["PT1"])
        mm(B[7][:], T.NIH[:], T.PT[:], ["NIH", "PT0", "PT1"], ["#7"], start=False)
        tt(TP, SP, T.NH[:], ALU.mult, ["NH", "#5"], ["#4"])

    def amend_s():
        tt(SP, TP, T.CR[:], ALU.max, ["#4", "CR"], ["#5"])

    def flags(c0, c1, far, bank):
        ts(T.CM[:, c0:c1], far, T.thF[:, 0:1], None, ALU.is_lt, None, [bank, "thF"], ["CM%d" % c0])
        ts(T.RB[:, c0:c1, 0], far, T.thF[:, 0:1], -8192.0, ALU.is_lt, ALU.mult, [bank, "thF", "RB0"], ["RBb%d" % c0])

    for r in range(RO):
        last = r == RO - 1
        MO, MI, BO, BI, CO, CN = (T[k + str(r)] for k in ("MO", "MI", "BO", "BI", "CO", "CN"))
        xm = ["Xm"] if r == 0 else ["X"]
        dma("y", [(T.XM[:, 1024:2048], X[:, P + 1024:P + 2048])], xm, ["XMc"])
        dma("y", [(T.XM[:, 2048:3072], X[:, P + 2048:P + 3072])], xm, ["XMd"])
        act(T.XM[:, 0:1024], X[:, P:P + 1024], ACT.Copy, xm, ["XMa"])
        cp(T.XM[:, 3072:ZC], X[:, P + 3072:P + ZC], xm, ["XMb"])
        act(T.XM[:, ZC:M], X[:, 0:W].indirect(T.trig16[:, ZC // 16:256]), ACT.Copy, ["X", "Xm", "trig16"], ["XMz"])
        if r > 0:
            pair_sums()
        zs = [(ZC, ZC + 512, B[1][:], "#1"), (ZC + 512, M, B[4][:, 0:256], "#4")]
        for a, b, ps, bank in zs:
            mm2(ps, T.IDN[:], T.XM[:, a:b], T.NIB[:], X[:, P + a:P + b], ["IDN", "NIB", "XMz", "X", "Xm"], [bank])
        if r == 0:
            clear_u()
        for k, (a, b, part) in enumerate(GCH):
            tt(T.D[:, a:b], X[:, 0:W].indirect(T.trig16[:, a // 16:b // 16]), T.XM[:, a:b], ALU.subtract,
               ["X", "Xm", "trig16", "XM" + part], ["D%d" % k])
            act(T.D[:, a:b], T.D[:, a:b], ACT.Abs, ["D%d" % k], ["D%d" % k])
            if k == 1:
                for u, w, ps, bank in zs:
                    act(T.D[:, u:w], ps, ACT.Abs, [bank], ["Dz" + bank])
            if b % 1024 == 0 or b == ZC:
                b = M if b == ZC else b
                a0 = b - 1024
                fold(B[3][:, 0:64] if b == 3072 else B[0][:, a0 // 16:b // 16], T.ZB, 0, lambda j: T.D[:, a0 + j:b:16],
                     ["ZB"] + (["Dz#1", "Dz#4"] if b == M else [])
                     + ["D%d" % h for h, (u, w, _p) in enumerate(GCH) if u >= a0 and w <= b],
                     ["#3"] if b == 3072 else ["#0"])
        if r == 0:
            ts(T.tmpI[:, 0:256], T.tgI[:], 4, None, ALU.arith_shift_right, None, ["tgI"], ["tmp0"])
            ts(T.tmpI[:, 256:512], T.tgI[:], 15, None, ALU.bitwise_and, None, ["tgI"], ["tmp1"])
            ts(T.PF[:, 0:256], T.tmpI[:, 0:256], -192.0, None, ALU.add, None, ["tmp0"], ["PF"])
            cp(T.PF[:, 256:512], T.tmpI[:, 256:512], ["tmp1"], ["PF1"])
        else:
            rounded(T["CN%d" % (r - 1)])
            amend_t()
            act(T.PF[:], B[7][:], ACT.Copy, ["#7"], ["PF", "PF1"])
        before("y", auxs, [])
        dma("y", [(T.AUX[2:128:16, :], T.PF[:, 0:256]), (T.AUX[3:128:16, :], T.PF[:, 256:512])], ["PF", "PF1"], ["AUXt"])
        flags(0, 128, B[0][:, 0:128], "#0")
        flags(192, 256, B[0][:, 192:256], "#0")
        scan(T.RB[:, 1:129, 1], T.CM[:, 0:128], T.CM[:, 0:128], 0.0, ["CM0"], ["RBa0"])
        flags(128, 192, B[3][:, 0:64], "#3")
        scan(T.RB[:, 129:257, 1], T.CM[:, 128:256], T.CM[:, 128:256], T.RB[:, 128:129, 1], ["CM128", "CM192", "RBa0"], ["RBa1"])
        rb = ["RB0", "RBa0", "RBa1", "RBb0", "RBb128", "RBb192"]
        mm(B[0][:, 256:512], T.TRI[:], T.CM[:], ["TRI", "CM0", "CM128", "CM192"], ["#0"])
        act(T.REL[:], B[0][:, 256:512], ACT.Copy, ["#0"], ["REL"], scale=-1.0 / 32.0)
        fold(B[1][:, 0:32], T.ZB, 0, lambda j: T.RB[:, j:256:16, :], ["ZB"] + rb, ["#1"])
        mm(B[3][:, 256:257], T.BLK[:], T.RB[:, 256:257, 1], ["BLK"] + rb, ["#3"])
        if r > 0:
            amend_s()
        else:
            ts(SP, T.srcI[:], 32.0, None, ALU.add, None, ["srcI"], ["#5"])
        cp(T.HB[:], SP, ["#5"], ["HB"])
        tt(T.LO[:], SP, T.HB[:], ALU.subtract, ["#5", "HB"], ["LO"])
        act(T.SL[:], SP, ACT.Copy, ["#5"], ["SL"])
        dma("y", [(T.AUX[1:128:16, :], T.LO[:]), (T.AUX[0:128:16, :], T.SL[:])], ["SL", "LO"], auxs)
        act(T.PB[:], T.PF[:], ACT.Copy, ["PF", "PF1"], ["PB"])
        scan(T.MP[:], T.CS[:], B[1][:, 0:32], 0.0, ["CS", "#1"], ["MP"])
        cp(T.mp16[:], T.MP[:, 1:32:2], ["MP"], ["mp16"])
        tt(T.WM[:, 0:MK + 256].indirect(T.mp16[:]), T.REL[:], T.CW[:], ALU.add, ["mp16", "REL", "CW"], ["WM"])
        scan(T.UF[:], T.INC[:], T.WM[:, 0:CAP], C[:, 5:6], ["INC", "WM", "c5"], ["UF"])
        fold(B[2][:, 0:64], T.ZH, 0, lambda j: T.UF[:, j:CAP:16], ["ZH", "UF"], ["#2"])
        ts(T.FL[:], T.KI[:], B[3][:, 256:257], 16384.0, ALU.is_ge, ALU.mult, ["KIa", "KIb", "#3"], ["FL"])
        fold(B[3][:, 0:64], T.ZH, 144, lambda j: T.UF[:, j:CAP:16], ["ZH", "UF"], ["#3"])
        if not last:
            act(T.WM[:, 0:CAP], T.WT[:], ACT.Copy, ["WT"], ["WM"])
        tt(DF, T.TL[:], SP, ALU.subtract, ["TL"], ["#5"])
        tt(T.TR[:], T.FL[:], T.KT[:], ALU.add, ["FL", "KTa", "KTb"], ["TR"])
        ts(T.pi16[:], B[2][:, 0:64], -4423552.0, 4095.0, ALU.add, ALU.min, ["#2"], ["pi16"])
        aux = auxs + ["pi16", "AUXt"]
        cp(T.GA[:, 0:H], T.AUX[:, 0:M].indirect(T.pi16[:, 0:32]), aux, ["GA0"])
        act(T.GA[:, H:CAP], T.AUX[:, 0:M].indirect(T.pi16[:, 32:64]), ACT.Copy, aux, ["GA1"])
        fold(B[4][:, 0:64], T.ZB, 144, lambda j: T.GA[:, j:CAP:16], ["ZBb", "GA0", "GA1"], ["#4"])
        fold(B[2][:, 0:64], T.ZB, 288, lambda j: T.GA[:, j:CAP:16], ["ZBb", "GA0", "GA1"], ["#2"])
        fold(B[1][:, 0:64], T.ZB, 432, lambda j: T.GA[:, j:CAP:16], ["ZBb", "GA0", "GA1"], ["#1"])
        ts(T.i16[:], B[3][:, 0:64], -15231.75, 4095.0, ALU.add, ALU.min, ["#3"], ["i16"])
        act(T.Q[:, 0:H], X[:, P:W].indirect(T.i16[:, 0:32]), ACT.Relu, ["X", "i16"], ["Q0"], bias=128.0, scale=-16.0)
        ts(T.Q[:, H:CAP], X[:, P:W].indirect(T.i16[:, 32:64]), 8.0, 16.0, ALU.is_lt, ALU.mult, ["X", "i16"], ["Q1"])
        act(T.GC[:], T.AUX[:, 0:M].indirect(T.pi16[:]), ACT.Copy, aux, ["GC"])
        ts(T.s16[:], B[4][:, 0:64], -32.0, None, ALU.add, None, ["#4"], ["s16"])
        for step, k in enumerate(SEND):
            a, b, far = PIECES[k]
            if step == 2:
                tt(T.BP[:, 0:64], B[2][:, 0:64], T.TR[:, 0:64], ALU.max, ["#2", "TR"], ["BPa"])
                ts(T.pos16[:], T.BP[:, 0:64], 192.0, None, ALU.add, None, ["BPa"], ["pos16"])
            if step == 3:
                tt(T.BP[:, 64:128], B[1][:, 0:64], T.TR[:, 64:128], ALU.max, ["#1", "TR"], ["BPb"])
                ts(BO[:], T.BP[:, 64:128], 3072.0, None, ALU.add, None, ["BPb"], ["BO"])
                post(dst, BI[:], BO[:], "ab%d" % r, ["BO"])
            tt(MO[:, a:b], X[:, 0:W].indirect(T.s16[:, a // 16:b // 16]), T.Q[:, a:b], ALU.max,
               ["X", "s16", "Q1" if a >= H else "Q0"], ["MO%d" % k])
            post(via if (far and via is not None) else dst, MI[:, a:b], MO[:, a:b], "am%d_%d" % (k, r), ["MO%d" % k])
        op("s", lambda: S.activation(T.U[:, 0:XW].indirect(T.pos16[:, 0:US // 16]), T.GC[:, 0:US], ACT.Silu),
           ["pos16", "GC"], ["U"])
        cp(T.U2[:, 0:XW].indirect(T.pos16[:, US // 16:64]), T.GC[:, US:CAP], ["pos16", "GC"], ["U2"])
        dma("y", [(CO[:, 0:384], T.U[0:128:16, 0:W])], ["U"], ["COa"])
        dma("y", [(CO[:, 384:768], T.U2[0:128:16, 0:W])], ["U2"], ["COb"])
        before("g", ["COa", "COb"], [])
        rid, pid, _se = topo.addr(dst)
        g.remote_dma_fused([RemoteDMATransfer(dst_ids=[DstId(rid=rid, pnc=pid)], dma_engine_mask=topo.mask(core, dst),
                                              remote_sem=T.sem["ac%d" % r], srcs=[CO[:, 128:384], CO[:, 512:768]],
                                              dsts=[CN[:]], alu_op=1)], local_sem=T.sem.sent)
        nsent[0] += len(topo.engines(core, dst))
        if not last:
            clear_u()
        arrives("BI", "ab%d" % r, frm)
        for k, (a, b, far) in enumerate(PIECES):
            arrives("MI%d" % k, "am%d_%d" % (k, r), via_in if (far and via_in is not None) else frm)
        win = X[:, 0:XW]
        act(T.A[:, H:CAP], win.indirect(BI[:, 32:64]), ACT.Copy, ["X", "Xt", "BI"], ["AS"])
        for k, (a, b, far) in enumerate(PIECES):
            ix = win.indirect(BI[:, a // 16:b // 16])
            mi = "MI%d" % k
            if a < H:
                if k == 0:
                    ts(T.A[:, a:b], MI[:, a:b], 16.0, 16.0, ALU.is_ge, ALU.mult, [mi], ["A%d" % k])
                else:
                    act(T.A[:, a:b], MI[:, a:b], ACT.Relu, [mi], ["A%d" % k], bias=-240.0, scale=16.0)
                act(T.VV[:, a:b], MI[:, a:b], ACT.Relu, [mi], ["VV%d" % k], bias=15.0, scale=-1.0)
                tt(T.TT[:, a:b], ix, T.A[:, a:b], ALU.min, ["X", "Xt", "BI", "A%d" % k], ["TT%d" % k])
            else:
                bank = 0 if k % 2 else 3
                mm2(B[bank][:, 0:b - a], T.IDN[:], T.A[:, a:b], T.I16[:], MI[:, a:b], ["IDN", "I16", "AS", mi], ["#%d" % bank])
                act(T.VV[:, a:b], MI[:, a:b], ACT.Relu, [mi], ["VV%d" % k], bias=15.0, scale=-1.0)
                act(T.TT[:, a:b], B[bank][:, 0:b - a], ACT.Relu, ["#%d" % bank], ["TT%d" % k], bias=-256.0)
            tt(ix, T.TT[:, a:b], T.VV[:, a:b], ALU.add, ["BI", "TT%d" % k, "VV%d" % k], ["X", "Xt"])
        if last:
            dma("y", [(T.yx[:], X[:, 0:W])], ["X"], ["yx"])
        arrives("CN", "ac%d" % r, frm)
        act(T.NH[:], CN[:], ACT.Relu, ["CN"], ["NH"], bias=1.0, scale=-1.0 / 16.0)
        if last:
            pair_sums()
            rounded(CN)
        tt(TP, DF, T.NH[:], ALU.mult, ["#5", "NH"], ["#4"])
        tt(T.TL[:], TP, T.SL[:], ALU.add, ["#4", "SL"], ["TL"])
        if not last:
            ts(T.trig16[:], T.TL[:], -32.0, None, ALU.add, None, ["TL"], ["trig16"])
    act(T.OT[:], T.TL[:], ACT.Identity, ["TL"], ["OT"], bias=-32.0)
    dma("s", [(T.ytrig[:], T.OT[:])], ["OT"], ["ytrig"])
    amend_t()
    amend_s()
    act(T.OS[:], SP, ACT.Identity, ["#5"], ["OS"], bias=-32.0)
    dma("s", [(T.ysrc[:], T.OS[:])], ["OS"], ["ysrc"])
    ts(T.CQ[:], B[7][:, 0:256], 16.0, 3072.0, ALU.mult, ALU.add, ["#7"], ["CQ"])
    tt(T.OG[:], B[7][:, 256:512], T.CQ[:], ALU.add, ["#7", "CQ"], ["OG"])
    dma("s", [(T.ytg[:], T.OG[:])], ["OG"], ["ytg"])
    for sem, c in count.items():
        need("g", (sem, c, {}))
    g.wait_ge(T.sem.sent, nsent[0])
